import numpy as np
import ml_dtypes


def mxq(x, axis, fmt="e4m3"):
    dtype, down = {"e4m3": (ml_dtypes.float8_e4m3fn, 7), "e5m2": (ml_dtypes.float8_e5m2, 14)}[fmt]
    v = np.moveaxis(np.asarray(x, np.float32).astype(ml_dtypes.bfloat16).astype(np.float64), axis, -1)
    blocks = v.reshape(v.shape[:-1] + (-1, 32))
    amax = np.abs(blocks).max(-1, keepdims=True)
    byte = np.maximum(np.where(amax > 0, np.frexp(amax)[1] - 1 + 127, 0) - down, 1)
    scale = np.exp2(byte - 127.0)
    codes = (blocks / scale).astype(np.float32).astype(dtype).astype(np.float64)
    return np.moveaxis((codes * scale).reshape(v.shape), -1, axis)


WIDE = False


def mx_kscale(k):
    if not WIDE:
        return np.ones(k)
    levels = np.array([10, -10, 5, -5, 0])
    if k % 512:
        return np.exp2(np.random.permutation(np.resize(levels, k // 32))).repeat(32)
    a = np.empty((k // 512, 16))
    for p in range(k // 512):
        a[p, :8] = np.random.permutation(np.resize(levels, 8))
        for g in range(8):
            far = levels[np.abs(levels - a[p, g]) >= 10]
            a[p, g + 8] = far[np.random.randint(len(far))]
    return np.exp2(a.ravel()).repeat(32)


def f64(x):
    return np.asarray(x).astype(np.float64)


def striped8(idx):
    return np.concatenate([v.reshape(-1, 16).T for v in idx]).astype(np.uint16)


def unstriped8(offs):
    return np.stack([offs[16 * g:16 * g + 16].T.reshape(-1) for g in range(8)]).astype(np.int64)


K, M, T, S = 512, 1024, 1024, 512


def setup_inputs():
    n = np.random.standard_normal
    s = mx_kscale(K)[:, None]
    return {
        "xT": (n((K, T)) * s).astype(np.float32),
        "w": (n((K, M)) / np.sqrt(K) / s).astype(np.float32),
        "wgt": np.repeat(np.random.uniform(0.5, 2.0, (8, S)), 16, axis=0).astype(np.float32),
        "wgo": np.repeat(np.random.uniform(0.5, 2.0, (8, S)), 16, axis=0).astype(np.float32),
        "offs": striped8(np.stack([np.random.permutation(T)[:S] for _ in range(8)])),
        "offs2": striped8(np.stack([np.random.permutation(T)[:S] for _ in range(8)])),
    }


def reference(xT, w, wgt, wgo, offs, offs2):
    idx = unstriped8(offs)
    group = np.arange(K) % 512 // 64
    xg = f64(wgt)[np.arange(K) // 4 % 128] * f64(xT)[np.arange(K)[:, None], idx[group]]
    xT_ = mxq(xg, 0, "e4m3")
    w_ = mxq(f64(w), 0, "e4m3")
    y = w_.T @ xT_
    place = unstriped8(offs2)[np.arange(M) % 128 // 16]
    out = np.zeros((M, T))
    out[np.arange(M)[:, None], place] = f64(wgo)[np.arange(M) % 128] * (y)
    return out

@@ -1,0 +1,169 @@
+import concourse.mybir as mybir
+
+K, M, T, S = 512, 1024, 1024, 512
+FLOPS = 2 * K * M * S
+
+F32 = mybir.dt.float32
+BF16 = mybir.dt.bfloat16
+U32 = mybir.dt.uint32
+U16 = mybir.dt.uint16
+U8 = mybir.dt.uint8
+FP8X4 = mybir.dt.float8_e4m3fn_x4
+MULT = mybir.AluOpType.mult
+
+P = 128
+PACK = 4
+HALF = S // 2
+LIST_COLS = S // 16
+HALF_COLS = LIST_COLS // 2
+BLOCKS = M // P
+
+
+def tile_list_hboth_none_kernel(tc, xT, w, wgt, wgo, offs, offs2, out):
+    nc = tc.nc
+    x_planes = xT.rearrange("(p i) t -> p i t", i=PACK)
+    w_rows = w.rearrange("(p i) n -> p i n", i=PACK)
+
+    with (
+        tc.tile_pool(name="held", bufs=1) as held,
+        tc.psum_pool(name="psum", bufs=1) as psum,
+    ):
+        list_in = held.tile([P, LIST_COLS], U16, name="list_in")
+        list_out = held.tile([P, LIST_COLS], U16, name="list_out")
+        wgt_half = [held.tile([P, HALF], F32, name=f"wgt{h}") for h in range(2)]
+        wgo_all = held.tile([P, S], F32, name="wgo_all")
+        planes = [held.tile([P, T], F32, name=f"plane{i}") for i in range(PACK)]
+        windows = [held.tile([P, T], F32, name=f"window{b}") for b in range(BLOCKS)]
+
+        nc.sync.dma_start(list_in[:], offs)
+        nc.scalar.dma_start(wgt_half[0][:], wgt[:, 0:HALF])
+        nc.sync.dma_start(planes[0][:], x_planes[:, 0, :])
+        nc.scalar.dma_start(wgt_half[1][:], wgt[:, HALF:S])
+        for i in range(1, PACK):
+            nc.sync.dma_start(planes[i][:], x_planes[:, i, :])
+
+        for b in range(6):
+            nc.vector.memset(windows[b][:], 0.0)
+        for b in range(6, BLOCKS):
+            nc.vector.memset(windows[b][:, 0:8], 0.0)
+        for b in range(6, BLOCKS):
+            nc.gpsimd.memset(windows[b][:], 0.0)
+
+        w_loads = [(0, 128), (128, 384), (512, 512)]
+        w_raw = []
+        for n, (c0, width) in enumerate(w_loads):
+            raw = held.tile([P, PACK, width], F32, name=f"w_raw{n}")
+            nc.sync.dma_start(raw[:], w_rows[:, :, c0 : c0 + width])
+            w_raw.append(raw)
+            if n == 0:
+                nc.sync.dma_start(list_out[:], offs2)
+                nc.sync.dma_start(wgo_all[:], wgo)
+
+        gathered = [held.tile([P, PACK, HALF], F32, name=f"gathered{h}") for h in range(2)]
+        x_grouped = [held.tile([P, HALF, PACK], BF16, align_bytes=64, name=f"x_grouped{h}") for h in range(2)]
+        x_codes = held.tile([P, S], U32, align_bytes=64, name="x_codes")
+        x_scales = held.tile([P, S], U8, align_bytes=64, name="x_scales")
+
+        def gather(i, h):
+            nc.vector.tensor_tensor(
+                gathered[h][:, i, :],
+                planes[i][:].indirect(list_in[:, h * HALF_COLS : (h + 1) * HALF_COLS]),
+                wgt_half[h][:],
+                MULT,
+            )
+
+        def interleave(copy, grouped, rows):
+            copy(
+                out=grouped.rearrange("p (c i) t -> p c t i", i=4),
+                in_=rows.rearrange("p t (c i) -> p c t i", i=4),
+            )
+
+        def quantize_x(h):
+            cols = slice(h * HALF, (h + 1) * HALF)
+            nc.vector.quantize_mx(
+                out=x_codes[:, cols].bitcast(FP8X4),
+                scales=x_scales[:, cols],
+                in_=x_grouped[h][:].rearrange("p c t -> p (c t)"),
+            )
+
+        w_codes = {}
+
+        def prepare_w(n, c0, width):
+            start = w_loads[n][0]
+            grouped = held.tile([P, width, PACK], BF16, align_bytes=64, name=f"w_grouped{c0}")
+            codes = held.tile([P, width], U32, align_bytes=64, name=f"w_codes{c0}")
+            scales = held.tile([P, width], U8, align_bytes=64, name=f"w_scales{c0}")
+            interleave(nc.scalar.copy, grouped[:], w_raw[n][:, :, c0 - start : c0 - start + width])
+            nc.vector.quantize_mx(
+                out=codes[:].bitcast(FP8X4),
+                scales=scales[:],
+                in_=grouped[:].rearrange("p c t -> p (c t)"),
+            )
+            for b in range(c0 // P, (c0 + width) // P):
+                cols = slice(b * P - c0, (b + 1) * P - c0)
+                w_codes[b] = (codes[:, cols].bitcast(FP8X4), scales[:, cols])
+
+        y = {}
+
+        def product(b, h0, h1):
+            cols = slice(h0 * HALF, h1 * HALF)
+            width = (h1 - h0) * HALF
+            bank = psum.tile([P, width], F32, name=f"bank{b % 4}_{h0}" if b < 2 else f"wide{b % 4}")
+            nc.tensor.matmul_mx(
+                out=bank[:],
+                lhsT=w_codes[b][0],
+                lhsT_scale=w_codes[b][1],
+                rhs=x_codes[:, cols].bitcast(FP8X4),
+                rhs_scale=x_scales[:, cols],
+                start=True,
+                stop=True,
+            )
+            rows = held.tile([P, width], F32, name=f"y{b}_{h0}")
+            nc.scalar.copy(out=rows[:], in_=bank[:])
+            for h in range(h0, h1):
+                y[b, h] = rows[:, (h - h0) * HALF : (h - h0 + 1) * HALF]
+
+        def scatter(b, h):
+            nc.vector.tensor_tensor(
+                windows[b][:].indirect(list_out[:, h * HALF_COLS : (h + 1) * HALF_COLS]),
+                y[b, h],
+                wgo_all[:, h * HALF : (h + 1) * HALF],
+                MULT,
+            )
+
+        def store(b):
+            nc.sync.dma_start(out[b * P : (b + 1) * P, :], windows[b][:])
+
+        def store_halves(b):
+            rows = slice(b * P, (b + 1) * P)
+            nc.sync.dma_start(out[rows, 0 : T // 2], windows[b][:, 0 : T // 2])
+            nc.scalar.dma_start(out[rows, T // 2 : T], windows[b][:, T // 2 : T])
+
+        for i, h in ((0, 0), (0, 1), (1, 0), (1, 1), (2, 0), (2, 1), (3, 0)):
+            gather(i, h)
+        interleave(nc.vector.tensor_copy, x_grouped[0][:], gathered[0][:])
+        prepare_w(0, 0, 128)
+        quantize_x(0)
+        gather(3, 1)
+        prepare_w(1, 128, 128)
+        product(0, 0, 1)
+        interleave(nc.scalar.copy, x_grouped[1][:], gathered[1][:])
+        product(1, 0, 1)
+        scatter(0, 0)
+        quantize_x(1)
+        scatter(1, 0)
+        product(0, 1, 2)
+        product(1, 1, 2)
+        prepare_w(1, 256, 256)
+        scatter(0, 1)
+        store(0)
+        product(2, 0, 2)
+        prepare_w(2, 512, 512)
+        for b in range(2, BLOCKS):
+            if b + 1 < BLOCKS:
+                product(b + 1, 0, 2)
+            scatter(b, 0)
+            scatter(b - 1, 1)
+            store(b - 1)
+        scatter(BLOCKS - 1, 1)
+        store_halves(BLOCKS - 1)

@@ -33,7 +33,8 @@ def tile_list_hboth_none_kernel(tc, xT, w, wgt, wgo, offs, offs2, out):
         wgt_half = [held.tile([P, HALF], F32, name=f"wgt{h}") for h in range(2)]
         wgo_all = held.tile([P, S], F32, name="wgo_all")
         planes = [held.tile([P, T], F32, name=f"plane{i}") for i in range(PACK)]
-        windows = [held.tile([P, T], F32, name=f"window{b}") for b in range(BLOCKS)]
+        windows = [held.tile([P, T], F32, name=f"window{b}") for b in range(4)]
+        windows = windows + windows
 
         nc.sync.dma_start(list_in[:], offs)
         nc.scalar.dma_start(wgt_half[0][:], wgt[:, 0:HALF])
@@ -42,12 +43,8 @@ def tile_list_hboth_none_kernel(tc, xT, w, wgt, wgo, offs, offs2, out):
         for i in range(1, PACK):
             nc.sync.dma_start(planes[i][:], x_planes[:, i, :])
 
-        for b in range(6):
+        for b in range(4):
             nc.vector.memset(windows[b][:], 0.0)
-        for b in range(6, BLOCKS):
-            nc.vector.memset(windows[b][:, 0:8], 0.0)
-        for b in range(6, BLOCKS):
-            nc.gpsimd.memset(windows[b][:], 0.0)
 
         w_loads = [(0, 128), (128, 384), (512, 512)]
         w_raw = []
@@ -120,6 +117,7 @@ def tile_list_hboth_none_kernel(tc, xT, w, wgt, wgo, offs, offs2, out):
             )
             rows = held.tile([P, width], F32, name=f"y{b}_{h0}")
             nc.scalar.copy(out=rows[:], in_=bank[:])
+            y[b] = rows[:]
             for h in range(h0, h1):
                 y[b, h] = rows[:, (h - h0) * HALF : (h - h0 + 1) * HALF]
 
@@ -130,6 +128,9 @@ def tile_list_hboth_none_kernel(tc, xT, w, wgt, wgo, offs, offs2, out):
                 wgo_all[:, h * HALF : (h + 1) * HALF],
                 MULT,
             )
+
+        def scatter_whole(b):
+            nc.vector.tensor_tensor(windows[b][:].indirect(list_out[:]), y[b], wgo_all[:], MULT)
 
         def store(b):
             nc.sync.dma_start(out[b * P : (b + 1) * P, :], windows[b][:])
@@ -159,11 +160,16 @@ def tile_list_hboth_none_kernel(tc, xT, w, wgt, wgo, offs, offs2, out):
         store(0)
         product(2, 0, 2)
         prepare_w(2, 512, 512)
-        for b in range(2, BLOCKS):
+        product(3, 0, 2)
+        scatter(2, 0)
+        scatter(1, 1)
+        store(1)
+        scatter(2, 1)
+        store(2)
+        for b in range(3, BLOCKS):
             if b + 1 < BLOCKS:
                 product(b + 1, 0, 2)
-            scatter(b, 0)
-            scatter(b - 1, 1)
-            store(b - 1)
-        scatter(BLOCKS - 1, 1)
+            scatter_whole(b)
+            if b + 1 < BLOCKS:
+                store(b)
         store_halves(BLOCKS - 1)

@@ -13,10 +13,10 @@ MULT = mybir.AluOpType.mult
 
 P = 128
 PACK = 4
-HALF = S // 2
-LIST_COLS = S // 16
-HALF_COLS = LIST_COLS // 2
+GROUP = 16
 BLOCKS = M // P
+WINDOWS = 4
+W_LOADS = ((0,128),(128,384),(512,512))
 
 
 def tile_list_hboth_none_kernel(tc, xT, w, wgt, wgo, offs, offs2, out):
@@ -28,44 +28,34 @@ def tile_list_hboth_none_kernel(tc, xT, w, wgt, wgo, offs, offs2, out):
         tc.tile_pool(name="held", bufs=1) as held,
         tc.psum_pool(name="psum", bufs=1) as psum,
     ):
-        list_in = held.tile([P, LIST_COLS], U16, name="list_in")
-        list_out = held.tile([P, LIST_COLS], U16, name="list_out")
-        wgt_half = [held.tile([P, HALF], F32, name=f"wgt{h}") for h in range(2)]
+        list_in = held.tile([P, S // GROUP], U16, name="list_in")
+        list_out = held.tile([P, S // GROUP], U16, name="list_out")
+        wgt_all = held.tile([P, S], F32, name="wgt_all")
         wgo_all = held.tile([P, S], F32, name="wgo_all")
         planes = [held.tile([P, T], F32, name=f"plane{i}") for i in range(PACK)]
-        windows = [held.tile([P, T], F32, name=f"window{b}") for b in range(4)]
-        windows = windows + windows
-
-        nc.sync.dma_start(list_in[:], offs)
-        nc.scalar.dma_start(wgt_half[0][:], wgt[:, 0:HALF])
-        nc.sync.dma_start(planes[0][:], x_planes[:, 0, :])
-        nc.scalar.dma_start(wgt_half[1][:], wgt[:, HALF:S])
-        for i in range(1, PACK):
-            nc.sync.dma_start(planes[i][:], x_planes[:, i, :])
-
-        for b in range(4):
-            nc.vector.memset(windows[b][:], 0.0)
-
-        w_loads = [(0, 128), (128, 384), (512, 512)]
-        w_raw = []
-        for n, (c0, width) in enumerate(w_loads):
-            raw = held.tile([P, PACK, width], F32, name=f"w_raw{n}")
-            nc.sync.dma_start(raw[:], w_rows[:, :, c0 : c0 + width])
-            w_raw.append(raw)
-            if n == 0:
-                nc.sync.dma_start(list_out[:], offs2)
-                nc.sync.dma_start(wgo_all[:], wgo)
-
-        gathered = [held.tile([P, PACK, HALF], F32, name=f"gathered{h}") for h in range(2)]
-        x_grouped = [held.tile([P, HALF, PACK], BF16, align_bytes=64, name=f"x_grouped{h}") for h in range(2)]
+        windows = [held.tile([P, T], F32, name=f"window{b}") for b in range(WINDOWS)]
+        w_raw = [held.tile([P, PACK, width], F32, name=f"w_raw{c0}") for c0, width in W_LOADS]
+        gathered = held.tile([P, PACK, S], F32, name="gathered")
+        x_grouped = held.tile([P, S, PACK], BF16, align_bytes=64, name="x_grouped")
         x_codes = held.tile([P, S], U32, align_bytes=64, name="x_codes")
         x_scales = held.tile([P, S], U8, align_bytes=64, name="x_scales")
+        w_grouped = held.tile([P, M, PACK], BF16, align_bytes=64, name="w_grouped")
+        w_codes = held.tile([P, M], U32, align_bytes=64, name="w_codes")
+        w_scales = held.tile([P, M], U8, align_bytes=64, name="w_scales")
+        y = [held.tile([P, S], F32, name=f"y{b}") for b in range(BLOCKS)]
 
-        def gather(i, h):
+        def load_w(n):
+            c0, width = W_LOADS[n]
+            nc.sync.dma_start(w_raw[n][:], w_rows[:, :, c0 : c0 + width])
+
+        def entries(list_tile, j0, j1):
+            return list_tile[:, j0 // GROUP : j1 // GROUP]
+
+        def gather(i, j0, j1):
             nc.vector.tensor_tensor(
-                gathered[h][:, i, :],
-                planes[i][:].indirect(list_in[:, h * HALF_COLS : (h + 1) * HALF_COLS]),
-                wgt_half[h][:],
+                gathered[:, i, j0:j1],
+                planes[i][:].indirect(entries(list_in, j0, j1)),
+                wgt_all[:, j0:j1],
                 MULT,
             )
 
@@ -75,101 +65,107 @@ def tile_list_hboth_none_kernel(tc, xT, w, wgt, wgo, offs, offs2, out):
                 in_=rows.rearrange("p t (c i) -> p c t i", i=4),
             )
 
-        def quantize_x(h):
-            cols = slice(h * HALF, (h + 1) * HALF)
+        def interleave_x(copy, j0, j1):
+            interleave(copy, x_grouped[:, j0:j1, :], gathered[:, :, j0:j1])
+
+        def interleave_w(copy, n0, n1):
+            n = max(m for m in range(len(W_LOADS)) if W_LOADS[m][0] <= n0)
+            c0 = W_LOADS[n][0]
+            interleave(copy, w_grouped[:, n0:n1, :], w_raw[n][:, :, n0 - c0 : n1 - c0])
+
+        def quantize(codes, scales, grouped, c0, c1):
             nc.vector.quantize_mx(
-                out=x_codes[:, cols].bitcast(FP8X4),
-                scales=x_scales[:, cols],
-                in_=x_grouped[h][:].rearrange("p c t -> p (c t)"),
+                out=codes[:, c0:c1].bitcast(FP8X4),
+                scales=scales[:, c0:c1],
+                in_=grouped[:, c0:c1, :].rearrange("p c t -> p (c t)"),
             )
 
-        w_codes = {}
+        def quantize_x(j0, j1):
+            quantize(x_codes, x_scales, x_grouped, j0, j1)
 
-        def prepare_w(n, c0, width):
-            start = w_loads[n][0]
-            grouped = held.tile([P, width, PACK], BF16, align_bytes=64, name=f"w_grouped{c0}")
-            codes = held.tile([P, width], U32, align_bytes=64, name=f"w_codes{c0}")
-            scales = held.tile([P, width], U8, align_bytes=64, name=f"w_scales{c0}")
-            interleave(nc.scalar.copy, grouped[:], w_raw[n][:, :, c0 - start : c0 - start + width])
-            nc.vector.quantize_mx(
-                out=codes[:].bitcast(FP8X4),
-                scales=scales[:],
-                in_=grouped[:].rearrange("p c t -> p (c t)"),
-            )
-            for b in range(c0 // P, (c0 + width) // P):
-                cols = slice(b * P - c0, (b + 1) * P - c0)
-                w_codes[b] = (codes[:, cols].bitcast(FP8X4), scales[:, cols])
+        def quantize_w(n0, n1):
+            quantize(w_codes, w_scales, w_grouped, n0, n1)
 
-        y = {}
-
-        def product(b, h0, h1):
-            cols = slice(h0 * HALF, h1 * HALF)
-            width = (h1 - h0) * HALF
-            bank = psum.tile([P, width], F32, name=f"bank{b % 4}_{h0}" if b < 2 else f"wide{b % 4}")
+        def product(b, j0, j1, bank_name, copy=nc.scalar.copy):
+            bank = psum.tile([P, j1 - j0], F32, name=bank_name)
+            rows = slice(b * P, (b + 1) * P)
             nc.tensor.matmul_mx(
                 out=bank[:],
-                lhsT=w_codes[b][0],
-                lhsT_scale=w_codes[b][1],
-                rhs=x_codes[:, cols].bitcast(FP8X4),
-                rhs_scale=x_scales[:, cols],
+                lhsT=w_codes[:, rows].bitcast(FP8X4),
+                lhsT_scale=w_scales[:, rows],
+                rhs=x_codes[:, j0:j1].bitcast(FP8X4),
+                rhs_scale=x_scales[:, j0:j1],
                 start=True,
                 stop=True,
             )
-            rows = held.tile([P, width], F32, name=f"y{b}_{h0}")
-            nc.scalar.copy(out=rows[:], in_=bank[:])
-            y[b] = rows[:]
-            for h in range(h0, h1):
-                y[b, h] = rows[:, (h - h0) * HALF : (h - h0 + 1) * HALF]
+            copy(out=y[b][:, j0:j1], in_=bank[:])
 
-        def scatter(b, h):
+        def scatter(b, j0, j1):
             nc.vector.tensor_tensor(
-                windows[b][:].indirect(list_out[:, h * HALF_COLS : (h + 1) * HALF_COLS]),
-                y[b, h],
-                wgo_all[:, h * HALF : (h + 1) * HALF],
+                windows[b % WINDOWS][:].indirect(entries(list_out, j0, j1)),
+                y[b][:, j0:j1],
+                wgo_all[:, j0:j1],
                 MULT,
             )
 
-        def scatter_whole(b):
-            nc.vector.tensor_tensor(windows[b][:].indirect(list_out[:]), y[b], wgo_all[:], MULT)
-
         def store(b):
-            nc.sync.dma_start(out[b * P : (b + 1) * P, :], windows[b][:])
+            nc.sync.dma_start(out[b * P : (b + 1) * P, :], windows[b % WINDOWS][:])
 
         def store_halves(b):
             rows = slice(b * P, (b + 1) * P)
-            nc.sync.dma_start(out[rows, 0 : T // 2], windows[b][:, 0 : T // 2])
-            nc.scalar.dma_start(out[rows, T // 2 : T], windows[b][:, T // 2 : T])
+            nc.sync.dma_start(out[rows, 0 : T // 2], windows[b % WINDOWS][:, 0 : T // 2])
+            nc.scalar.dma_start(out[rows, T // 2 : T], windows[b % WINDOWS][:, T // 2 : T])
 
-        for i, h in ((0, 0), (0, 1), (1, 0), (1, 1), (2, 0), (2, 1), (3, 0)):
-            gather(i, h)
-        interleave(nc.vector.tensor_copy, x_grouped[0][:], gathered[0][:])
-        prepare_w(0, 0, 128)
-        quantize_x(0)
-        gather(3, 1)
-        prepare_w(1, 128, 128)
-        product(0, 0, 1)
-        interleave(nc.scalar.copy, x_grouped[1][:], gathered[1][:])
-        product(1, 0, 1)
-        scatter(0, 0)
-        quantize_x(1)
-        scatter(1, 0)
-        product(0, 1, 2)
-        product(1, 1, 2)
-        prepare_w(1, 256, 256)
-        scatter(0, 1)
+        nc.sync.dma_start(list_in[:], offs)
+        nc.scalar.dma_start(wgt_all[:, 0:256], wgt[:, 0:256])
+        nc.sync.dma_start(planes[0][:], x_planes[:, 0, :])
+        nc.scalar.dma_start(wgt_all[:, 256:S], wgt[:, 256:S])
+        for i in range(1, PACK):
+            nc.sync.dma_start(planes[i][:], x_planes[:, i, :])
+        load_w(0)
+        nc.sync.dma_start(list_out[:], offs2)
+        nc.sync.dma_start(wgo_all[:], wgo)
+        load_w(1)
+        load_w(2)
+
+        for window in windows:
+            nc.vector.memset(window[:], 0.0)
+
+        V, A = nc.vector.tensor_copy, nc.scalar.copy
+        gather(0, 0, 256)
+        gather(0, 256, S)
+        gather(1, 0, S)
+        gather(2, 0, S)
+        gather(3, 0, 256)
+        interleave_x(V, 0, 256)
+        interleave_w(A, 0, 128)
+        quantize_w(0, 128)
+        quantize_x(0, 256)
+        gather(3, 256, S)
+        interleave_w(A, 128, 256)
+        quantize_w(128, 256)
+        product(0, 0, 256, "bank0")
+        interleave_x(A, 256, S)
+        product(1, 0, 256, "bank1")
+        scatter(0, 0, 256)
+        quantize_x(256, S)
+        scatter(1, 0, 256)
+        product(0, 256, S, "bank2")
+        product(1, 256, S, "bank3")
+        interleave_w(A, 256, 512)
+        quantize_w(256, 512)
+        scatter(0, 256, S)
         store(0)
-        product(2, 0, 2)
-        prepare_w(2, 512, 512)
-        product(3, 0, 2)
-        scatter(2, 0)
-        scatter(1, 1)
+        product(2, 0, S, "bank4")
+        interleave_w(A, 512, 1024)
+        quantize_w(512, 1024)
+        product(3, 0, S, "bank5")
+        scatter(1, 256, S)
         store(1)
-        scatter(2, 1)
-        store(2)
-        for b in range(3, BLOCKS):
-            if b + 1 < BLOCKS:
-                product(b + 1, 0, 2)
-            scatter_whole(b)
+        for b in range(2, BLOCKS):
+            if b + 2 < BLOCKS:
+                product(b + 2, 0, S, f"bank{4 + (b + 2) % 4}")
+            scatter(b, 0, S)
             if b + 1 < BLOCKS:
                 store(b)
         store_halves(BLOCKS - 1)

@@ -15,8 +15,8 @@ P = 128
 PACK = 4
 GROUP = 16
 BLOCKS = M // P
-WINDOWS = 4
-W_LOADS = ((0,128),(128,384),(512,512))
+WINDOWS = 3
+W_LOADS = ((0, 128), (128, 128), (256, 256), (512, 512))
 
 
 def tile_list_hboth_none_kernel(tc, xT, w, wgt, wgo, offs, offs2, out):
@@ -35,7 +35,8 @@ def tile_list_hboth_none_kernel(tc, xT, w, wgt, wgo, offs, offs2, out):
         planes = [held.tile([P, T], F32, name=f"plane{i}") for i in range(PACK)]
         windows = [held.tile([P, T], F32, name=f"window{b}") for b in range(WINDOWS)]
         w_raw = [held.tile([P, PACK, width], F32, name=f"w_raw{c0}") for c0, width in W_LOADS]
-        gathered = held.tile([P, PACK, S], F32, name="gathered")
+        gathered_row = held.tile([P, PACK * S + 256], F32, align_bytes=64, name="gathered")
+        gathered = gathered_row[:, 0 : PACK * S].rearrange("p (t j) -> p t j", t=PACK)
         x_grouped = held.tile([P, S, PACK], BF16, align_bytes=64, name="x_grouped")
         x_codes = held.tile([P, S], U32, align_bytes=64, name="x_codes")
         x_scales = held.tile([P, S], U8, align_bytes=64, name="x_scales")
@@ -43,6 +44,22 @@ def tile_list_hboth_none_kernel(tc, xT, w, wgt, wgo, offs, offs2, out):
         w_codes = held.tile([P, M], U32, align_bytes=64, name="w_codes")
         w_scales = held.tile([P, M], U8, align_bytes=64, name="w_scales")
         y = [held.tile([P, S], F32, name=f"y{b}") for b in range(BLOCKS)]
+
+        def w_stage(n0, n1):
+            return w_grouped[:, n0:n1, :]
+
+        def x_stage(j0, j1):
+            if j1 <= 256:
+                first = gathered_row[:, PACK * S - 256 : PACK * S + 256].bitcast(BF16)
+                return first[:, PACK * j0 : PACK * j1].rearrange("p (c t) -> p c t", t=PACK)
+            return x_grouped[:, j0:j1, :]
+
+        def y_part(b, j0, j1):
+            if b == 3:
+                return w_raw[3][:, 3, :]
+            if (b, j0) == (1, 256):
+                return w_raw[2][:, 3, :]
+            return y[b][:, j0:j1]
 
         def load_w(n):
             c0, width = W_LOADS[n]
@@ -66,25 +83,25 @@ def tile_list_hboth_none_kernel(tc, xT, w, wgt, wgo, offs, offs2, out):
             )
 
         def interleave_x(copy, j0, j1):
-            interleave(copy, x_grouped[:, j0:j1, :], gathered[:, :, j0:j1])
+            interleave(copy, x_stage(j0, j1), gathered[:, :, j0:j1])
 
         def interleave_w(copy, n0, n1):
             n = max(m for m in range(len(W_LOADS)) if W_LOADS[m][0] <= n0)
             c0 = W_LOADS[n][0]
-            interleave(copy, w_grouped[:, n0:n1, :], w_raw[n][:, :, n0 - c0 : n1 - c0])
+            interleave(copy, w_stage(n0, n1), w_raw[n][:, :, n0 - c0 : n1 - c0])
 
         def quantize(codes, scales, grouped, c0, c1):
             nc.vector.quantize_mx(
                 out=codes[:, c0:c1].bitcast(FP8X4),
                 scales=scales[:, c0:c1],
-                in_=grouped[:, c0:c1, :].rearrange("p c t -> p (c t)"),
+                in_=grouped.rearrange("p c t -> p (c t)"),
             )
 
         def quantize_x(j0, j1):
-            quantize(x_codes, x_scales, x_grouped, j0, j1)
+            quantize(x_codes, x_scales, x_stage(j0, j1), j0, j1)
 
         def quantize_w(n0, n1):
-            quantize(w_codes, w_scales, w_grouped, n0, n1)
+            quantize(w_codes, w_scales, w_stage(n0, n1), n0, n1)
 
         def product(b, j0, j1, bank_name, copy=nc.scalar.copy):
             bank = psum.tile([P, j1 - j0], F32, name=bank_name)
@@ -98,12 +115,12 @@ def tile_list_hboth_none_kernel(tc, xT, w, wgt, wgo, offs, offs2, out):
                 start=True,
                 stop=True,
             )
-            copy(out=y[b][:, j0:j1], in_=bank[:])
+            copy(out=y_part(b, j0, j1), in_=bank[:])
 
         def scatter(b, j0, j1):
             nc.vector.tensor_tensor(
                 windows[b % WINDOWS][:].indirect(entries(list_out, j0, j1)),
-                y[b][:, j0:j1],
+                y_part(b, j0, j1),
                 wgo_all[:, j0:j1],
                 MULT,
             )
@@ -123,10 +140,11 @@ def tile_list_hboth_none_kernel(tc, xT, w, wgt, wgo, offs, offs2, out):
         for i in range(1, PACK):
             nc.sync.dma_start(planes[i][:], x_planes[:, i, :])
         load_w(0)
+        load_w(1)
         nc.sync.dma_start(list_out[:], offs2)
         nc.sync.dma_start(wgo_all[:], wgo)
-        load_w(1)
         load_w(2)
+        load_w(3)
 
         for window in windows:
             nc.vector.memset(window[:], 0.0)
@@ -137,29 +155,30 @@ def tile_list_hboth_none_kernel(tc, xT, w, wgt, wgo, offs, offs2, out):
         gather(1, 0, S)
         gather(2, 0, S)
         gather(3, 0, 256)
-        interleave_x(V, 0, 256)
-        interleave_w(A, 0, 128)
-        quantize_w(0, 128)
-        quantize_x(0, 256)
-        gather(3, 256, S)
+        interleave_x(V, 0, 128)
+        interleave_x(A, 128, 256)
+        interleave_w(V, 0, 128)
         interleave_w(A, 128, 256)
-        quantize_w(128, 256)
+        quantize_x(0, 256)
+        quantize_w(0, 128)
         product(0, 0, 256, "bank0")
-        interleave_x(A, 256, S)
+        gather(3, 256, S)
+        quantize_w(128, 256)
         product(1, 0, 256, "bank1")
+        interleave_x(A, 256, S)
         scatter(0, 0, 256)
         quantize_x(256, S)
         scatter(1, 0, 256)
         product(0, 256, S, "bank2")
-        product(1, 256, S, "bank3")
         interleave_w(A, 256, 512)
+        product(1, 256, S, "bank3")
         quantize_w(256, 512)
         scatter(0, 256, S)
         store(0)
         product(2, 0, S, "bank4")
         interleave_w(A, 512, 1024)
-        quantize_w(512, 1024)
         product(3, 0, S, "bank5")
+        quantize_w(512, 1024)
         scatter(1, 256, S)
         store(1)
         for b in range(2, BLOCKS):

@@ -140,10 +140,11 @@ def tile_list_hboth_none_kernel(tc, xT, w, wgt, wgo, offs, offs2, out):
         for i in range(1, PACK):
             nc.sync.dma_start(planes[i][:], x_planes[:, i, :])
         load_w(0)
-        load_w(1)
         nc.sync.dma_start(list_out[:], offs2)
-        nc.sync.dma_start(wgo_all[:], wgo)
+        nc.sync.dma_start(wgo_all[:, 0:256], wgo[:, 0:256])
+        load_w(1)
         load_w(2)
+        nc.sync.dma_start(wgo_all[:, 256:S], wgo[:, 256:S])
         load_w(3)
 
         for window in windows:

@@ -133,9 +133,9 @@ def tile_list_hboth_none_kernel(tc, xT, w, wgt, wgo, offs, offs2, out):
             nc.sync.dma_start(out[rows, 0 : T // 2], windows[b % WINDOWS][:, 0 : T // 2])
             nc.scalar.dma_start(out[rows, T // 2 : T], windows[b % WINDOWS][:, T // 2 : T])
 
-        nc.sync.dma_start(list_in[:], offs)
-        nc.scalar.dma_start(wgt_all[:, 0:256], wgt[:, 0:256])
         nc.sync.dma_start(planes[0][:], x_planes[:, 0, :])
+        nc.scalar.dma_start(wgt_all[:, 0:256], wgt[:, 0:256])
+        nc.sync.dma_start(list_in[:], offs)
         nc.scalar.dma_start(wgt_all[:, 256:S], wgt[:, 256:S])
         for i in range(1, PACK):
             nc.sync.dma_start(planes[i][:], x_planes[:, i, :])

@@ -134,9 +134,8 @@ def tile_list_hboth_none_kernel(tc, xT, w, wgt, wgo, offs, offs2, out):
             nc.scalar.dma_start(out[rows, T // 2 : T], windows[b % WINDOWS][:, T // 2 : T])
 
         nc.sync.dma_start(planes[0][:], x_planes[:, 0, :])
-        nc.scalar.dma_start(wgt_all[:, 0:256], wgt[:, 0:256])
+        nc.scalar.dma_start(wgt_all[:], wgt)
         nc.sync.dma_start(list_in[:], offs)
-        nc.scalar.dma_start(wgt_all[:, 256:S], wgt[:, 256:S])
         for i in range(1, PACK):
             nc.sync.dma_start(planes[i][:], x_planes[:, i, :])
         load_w(0)
@@ -151,11 +150,11 @@ def tile_list_hboth_none_kernel(tc, xT, w, wgt, wgo, offs, offs2, out):
             nc.vector.memset(window[:], 0.0)
 
         V, A = nc.vector.tensor_copy, nc.scalar.copy
-        gather(0, 0, 256)
-        gather(0, 256, S)
+        gather(0, 0, S)
         gather(1, 0, S)
         gather(2, 0, S)
-        gather(3, 0, 256)
+        gather(3, 0, 128)
+        gather(3, 128, 256)
         interleave_x(V, 0, 128)
         interleave_x(A, 128, 256)
         interleave_w(V, 0, 128)

@@ -139,9 +139,9 @@ def tile_list_hboth_none_kernel(tc, xT, w, wgt, wgo, offs, offs2, out):
         for i in range(1, PACK):
             nc.sync.dma_start(planes[i][:], x_planes[:, i, :])
         load_w(0)
+        load_w(1)
         nc.sync.dma_start(list_out[:], offs2)
         nc.sync.dma_start(wgo_all[:, 0:256], wgo[:, 0:256])
-        load_w(1)
         load_w(2)
         nc.sync.dma_start(wgo_all[:, 256:S], wgo[:, 256:S])
         load_w(3)

@@ -16,6 +16,8 @@ PACK = 4
 GROUP = 16
 BLOCKS = M // P
 WINDOWS = 3
+BANKS = 8
+Q = 128
 W_LOADS = ((0, 128), (128, 128), (256, 256), (512, 512))
 
 
@@ -34,36 +36,39 @@ def tile_list_hboth_none_kernel(tc, xT, w, wgt, wgo, offs, offs2, out):
         wgo_all = held.tile([P, S], F32, name="wgo_all")
         planes = [held.tile([P, T], F32, name=f"plane{i}") for i in range(PACK)]
         windows = [held.tile([P, T], F32, name=f"window{b}") for b in range(WINDOWS)]
-        w_raw = [held.tile([P, PACK, width], F32, name=f"w_raw{c0}") for c0, width in W_LOADS]
-        gathered_row = held.tile([P, PACK * S + 256], F32, align_bytes=64, name="gathered")
+        gathered_row = held.tile([P, PACK * S + 3 * Q], F32, align_bytes=64, name="gathered")
         gathered = gathered_row[:, 0 : PACK * S].rearrange("p (t j) -> p t j", t=PACK)
-        x_grouped = held.tile([P, S, PACK], BF16, align_bytes=64, name="x_grouped")
-        x_codes = held.tile([P, S], U32, align_bytes=64, name="x_codes")
-        x_scales = held.tile([P, S], U8, align_bytes=64, name="x_scales")
-        w_grouped = held.tile([P, M, PACK], BF16, align_bytes=64, name="w_grouped")
-        w_codes = held.tile([P, M], U32, align_bytes=64, name="w_codes")
-        w_scales = held.tile([P, M], U8, align_bytes=64, name="w_scales")
-        y = [held.tile([P, S], F32, name=f"y{b}") for b in range(BLOCKS)]
+        w_first = gathered_row[:, PACK * S - Q : PACK * S + 3 * Q].rearrange("p (t n) -> p t n", t=PACK)
+        w_raw = [w_first] + [
+            held.tile([P, PACK, width], F32, name=f"w_raw{c0}")[:] for c0, width in W_LOADS[1:]
+        ]
+        staging = held.tile([P, 4 * Q * PACK], BF16, align_bytes=64, name="staging")
+        codes = held.tile([P, S + M], U32, align_bytes=64, name="codes")
+        scales = held.tile([P, S + M], U8, align_bytes=64, name="scales")
+        y = {b: held.tile([P, S], F32, name=f"y{b}") for b in range(BLOCKS) if b != 3}
 
-        def w_stage(n0, n1):
-            return w_grouped[:, n0:n1, :]
+        def stage(u0, u1):
+            return staging[:, u0 * Q * PACK : u1 * Q * PACK]
 
-        def x_stage(j0, j1):
-            if j1 <= 256:
-                first = gathered_row[:, PACK * S - 256 : PACK * S + 256].bitcast(BF16)
-                return first[:, PACK * j0 : PACK * j1].rearrange("p (c t) -> p c t", t=PACK)
-            return x_grouped[:, j0:j1, :]
+        def x_cols(j0, j1):
+            return slice(Q + j0, Q + j1)
+
+        def w_cols(n0, n1):
+            shift = 0 if n0 == 0 else S
+            return slice(shift + n0, shift + n1)
 
         def y_part(b, j0, j1):
             if b == 3:
                 return w_raw[3][:, 3, :]
-            if (b, j0) == (1, 256):
+            if (b, j0) == (1, 2 * Q):
                 return w_raw[2][:, 3, :]
+            if (b, j0) == (0, 3 * Q):
+                return w_raw[2][:, 2, Q : 2 * Q]
             return y[b][:, j0:j1]
 
         def load_w(n):
             c0, width = W_LOADS[n]
-            nc.sync.dma_start(w_raw[n][:], w_rows[:, :, c0 : c0 + width])
+            nc.sync.dma_start(w_raw[n], w_rows[:, :, c0 : c0 + width])
 
         def entries(list_tile, j0, j1):
             return list_tile[:, j0 // GROUP : j1 // GROUP]
@@ -76,46 +81,40 @@ def tile_list_hboth_none_kernel(tc, xT, w, wgt, wgo, offs, offs2, out):
                 MULT,
             )
 
-        def interleave(copy, grouped, rows):
+        def interleave(copy, staged, rows):
             copy(
-                out=grouped.rearrange("p (c i) t -> p c t i", i=4),
+                out=staged.rearrange("p (c i t) -> p c t i", i=4, t=PACK),
                 in_=rows.rearrange("p t (c i) -> p c t i", i=4),
             )
 
-        def interleave_x(copy, j0, j1):
-            interleave(copy, x_stage(j0, j1), gathered[:, :, j0:j1])
+        def interleave_x(copy, unit, j0):
+            interleave(copy, stage(unit, unit + 1), gathered[:, :, j0 : j0 + Q])
 
-        def interleave_w(copy, n0, n1):
+        def interleave_w(copy, unit, n0, n1):
             n = max(m for m in range(len(W_LOADS)) if W_LOADS[m][0] <= n0)
             c0 = W_LOADS[n][0]
-            interleave(copy, w_stage(n0, n1), w_raw[n][:, :, n0 - c0 : n1 - c0])
+            interleave(copy, stage(unit, unit + (n1 - n0) // Q), w_raw[n][:, :, n0 - c0 : n1 - c0])
 
-        def quantize(codes, scales, grouped, c0, c1):
+        def quantize(unit, c0, c1):
             nc.vector.quantize_mx(
                 out=codes[:, c0:c1].bitcast(FP8X4),
                 scales=scales[:, c0:c1],
-                in_=grouped.rearrange("p c t -> p (c t)"),
+                in_=stage(unit, unit + (c1 - c0) // Q),
             )
 
-        def quantize_x(j0, j1):
-            quantize(x_codes, x_scales, x_stage(j0, j1), j0, j1)
-
-        def quantize_w(n0, n1):
-            quantize(w_codes, w_scales, w_stage(n0, n1), n0, n1)
-
-        def product(b, j0, j1, bank_name, copy=nc.scalar.copy):
-            bank = psum.tile([P, j1 - j0], F32, name=bank_name)
-            rows = slice(b * P, (b + 1) * P)
+        def product(b, j0, j1, bank_number):
+            bank = psum.tile([P, j1 - j0], F32, name=f"bank{bank_number % BANKS}")
+            rows = w_cols(b * P, (b + 1) * P)
             nc.tensor.matmul_mx(
                 out=bank[:],
-                lhsT=w_codes[:, rows].bitcast(FP8X4),
-                lhsT_scale=w_scales[:, rows],
-                rhs=x_codes[:, j0:j1].bitcast(FP8X4),
-                rhs_scale=x_scales[:, j0:j1],
+                lhsT=codes[:, rows].bitcast(FP8X4),
+                lhsT_scale=scales[:, rows],
+                rhs=codes[:, x_cols(j0, j1)].bitcast(FP8X4),
+                rhs_scale=scales[:, x_cols(j0, j1)],
                 start=True,
                 stop=True,
             )
-            copy(out=y_part(b, j0, j1), in_=bank[:])
+            nc.scalar.copy(out=y_part(b, j0, j1), in_=bank[:])
 
         def scatter(b, j0, j1):
             nc.vector.tensor_tensor(
@@ -139,11 +138,11 @@ def tile_list_hboth_none_kernel(tc, xT, w, wgt, wgo, offs, offs2, out):
         for i in range(1, PACK):
             nc.sync.dma_start(planes[i][:], x_planes[:, i, :])
         load_w(0)
-        load_w(1)
         nc.sync.dma_start(list_out[:], offs2)
-        nc.sync.dma_start(wgo_all[:, 0:256], wgo[:, 0:256])
+        nc.sync.dma_start(wgo_all[:, 0 : 3 * Q], wgo[:, 0 : 3 * Q])
+        load_w(1)
         load_w(2)
-        nc.sync.dma_start(wgo_all[:, 256:S], wgo[:, 256:S])
+        nc.sync.dma_start(wgo_all[:, 3 * Q : S], wgo[:, 3 * Q : S])
         load_w(3)
 
         for window in windows:
@@ -153,37 +152,45 @@ def tile_list_hboth_none_kernel(tc, xT, w, wgt, wgo, offs, offs2, out):
         gather(0, 0, S)
         gather(1, 0, S)
         gather(2, 0, S)
-        gather(3, 0, 128)
-        gather(3, 128, 256)
-        interleave_x(V, 0, 128)
-        interleave_x(A, 128, 256)
-        interleave_w(V, 0, 128)
-        interleave_w(A, 128, 256)
-        quantize_x(0, 256)
-        quantize_w(0, 128)
-        product(0, 0, 256, "bank0")
-        gather(3, 256, S)
-        quantize_w(128, 256)
-        product(1, 0, 256, "bank1")
-        interleave_x(A, 256, S)
-        scatter(0, 0, 256)
-        quantize_x(256, S)
-        scatter(1, 0, 256)
-        product(0, 256, S, "bank2")
-        interleave_w(A, 256, 512)
-        product(1, 256, S, "bank3")
-        quantize_w(256, 512)
-        scatter(0, 256, S)
+        gather(3, 0, Q)
+        gather(3, Q, 2 * Q)
+        gather(3, 2 * Q, 3 * Q)
+        interleave_x(A, 1, 0)
+        interleave_x(A, 2, Q)
+        interleave_x(A, 3, 2 * Q)
+        interleave_w(V, 0, 0, Q)
+        gather(3, 3 * Q, S)
+        quantize(0, 0, 2 * Q)
+        product(0, 0, Q, 0)
+        interleave_x(V, 1, 3 * Q)
+        quantize(2, 2 * Q, 4 * Q)
+        interleave_w(A, 2, Q, 2 * Q)
+        product(0, Q, 3 * Q, 1)
+        scatter(0, 0, Q)
+        quantize(1, 4 * Q, 6 * Q)
+        scatter(0, Q, 3 * Q)
+        product(1, 0, 2 * Q, 2)
+        interleave_w(A, 1, 2 * Q, 3 * Q)
+        interleave_w(A, 2, 3 * Q, 4 * Q)
+        product(0, 3 * Q, S, 3)
+        product(1, 2 * Q, S, 4)
+        scatter(1, 0, 2 * Q)
+        quantize(1, 6 * Q, 8 * Q)
+        scatter(0, 3 * Q, S)
         store(0)
-        product(2, 0, S, "bank4")
-        interleave_w(A, 512, 1024)
-        product(3, 0, S, "bank5")
-        quantize_w(512, 1024)
-        scatter(1, 256, S)
+        product(2, 0, S, 5)
+        interleave_w(A, 0, 4 * Q, 6 * Q)
+        interleave_w(A, 2, 6 * Q, 8 * Q)
+        product(3, 0, S, 6)
+        scatter(1, 2 * Q, S)
         store(1)
-        for b in range(2, BLOCKS):
+        scatter(2, 0, S)
+        store(2)
+        quantize(0, 8 * Q, 12 * Q)
+        product(4, 0, S, 7)
+        for b in range(3, BLOCKS):
             if b + 2 < BLOCKS:
-                product(b + 2, 0, S, f"bank{4 + (b + 2) % 4}")
+                product(b + 2, 0, S, b + 5)
             scatter(b, 0, S)
             if b + 1 < BLOCKS:
                 store(b)

@@ -127,11 +127,6 @@ def tile_list_hboth_none_kernel(tc, xT, w, wgt, wgo, offs, offs2, out):
         def store(b):
             nc.sync.dma_start(out[b * P : (b + 1) * P, :], windows[b % WINDOWS][:])
 
-        def store_halves(b):
-            rows = slice(b * P, (b + 1) * P)
-            nc.sync.dma_start(out[rows, 0 : T // 2], windows[b % WINDOWS][:, 0 : T // 2])
-            nc.scalar.dma_start(out[rows, T // 2 : T], windows[b % WINDOWS][:, T // 2 : T])
-
         nc.sync.dma_start(planes[0][:], x_planes[:, 0, :])
         nc.scalar.dma_start(wgt_all[:], wgt)
         nc.sync.dma_start(list_in[:], offs)
@@ -192,6 +187,4 @@ def tile_list_hboth_none_kernel(tc, xT, w, wgt, wgo, offs, offs2, out):
             if b + 2 < BLOCKS:
                 product(b + 2, 0, S, b + 5)
             scatter(b, 0, S)
-            if b + 1 < BLOCKS:
-                store(b)
-        store_halves(BLOCKS - 1)
+            store(b)

@@ -36,9 +36,9 @@ def tile_list_hboth_none_kernel(tc, xT, w, wgt, wgo, offs, offs2, out):
         wgo_all = held.tile([P, S], F32, name="wgo_all")
         planes = [held.tile([P, T], F32, name=f"plane{i}") for i in range(PACK)]
         windows = [held.tile([P, T], F32, name=f"window{b}") for b in range(WINDOWS)]
-        gathered_row = held.tile([P, PACK * S + 3 * Q], F32, align_bytes=64, name="gathered")
+        gathered_row = held.tile([P, PACK * S + 4 * Q - Q // 2], F32, align_bytes=64, name="gathered")
         gathered = gathered_row[:, 0 : PACK * S].rearrange("p (t j) -> p t j", t=PACK)
-        w_first = gathered_row[:, PACK * S - Q : PACK * S + 3 * Q].rearrange("p (t n) -> p t n", t=PACK)
+        w_first = gathered_row[:, PACK * S - Q // 2 : PACK * S + 4 * Q - Q // 2].rearrange("p (t n) -> p t n", t=PACK)
         w_raw = [w_first] + [
             held.tile([P, PACK, width], F32, name=f"w_raw{c0}")[:] for c0, width in W_LOADS[1:]
         ]
@@ -151,9 +151,10 @@ def tile_list_hboth_none_kernel(tc, xT, w, wgt, wgo, offs, offs2, out):
         gather(3, Q, 2 * Q)
         gather(3, 2 * Q, 3 * Q)
         interleave_x(A, 1, 0)
+        interleave(A, staging[:, Q * PACK // 2 : Q * PACK], w_first[:, :, Q // 2 : Q])
         interleave_x(A, 2, Q)
         interleave_x(A, 3, 2 * Q)
-        interleave_w(V, 0, 0, Q)
+        interleave(V, staging[:, 0 : Q * PACK // 2], w_first[:, :, 0 : Q // 2])
         gather(3, 3 * Q, S)
         quantize(0, 0, 2 * Q)
         product(0, 0, Q, 0)

@@ -90,6 +90,12 @@ def tile_list_hboth_none_kernel(tc, xT, w, wgt, wgo, offs, offs2, out):
         def interleave_x(copy, unit, j0):
             interleave(copy, stage(unit, unit + 1), gathered[:, :, j0 : j0 + Q])
 
+        def interleave_pair(t0, unit, j0, j1):
+            nc.scalar.copy(
+                out=stage(unit, unit + (j1 - j0) // Q).rearrange("p (c i t) -> p c t i", i=4, t=PACK)[:, :, t0 : t0 + 2, :],
+                in_=gathered[:, t0 : t0 + 2, j0:j1].rearrange("p t (c i) -> p c t i", i=4),
+            )
+
         def interleave_w(copy, unit, n0, n1):
             n = max(m for m in range(len(W_LOADS)) if W_LOADS[m][0] <= n0)
             c0 = W_LOADS[n][0]
@@ -146,14 +152,15 @@ def tile_list_hboth_none_kernel(tc, xT, w, wgt, wgo, offs, offs2, out):
         V, A = nc.vector.tensor_copy, nc.scalar.copy
         gather(0, 0, S)
         gather(1, 0, S)
+        interleave_pair(0, 1, 0, 3 * Q)
         gather(2, 0, S)
         gather(3, 0, Q)
         gather(3, Q, 2 * Q)
         gather(3, 2 * Q, 3 * Q)
-        interleave_x(A, 1, 0)
+        interleave_pair(2, 1, 0, Q)
         interleave(A, staging[:, Q * PACK // 2 : Q * PACK], w_first[:, :, Q // 2 : Q])
-        interleave_x(A, 2, Q)
-        interleave_x(A, 3, 2 * Q)
+        interleave_pair(2, 2, Q, 2 * Q)
+        interleave_pair(2, 3, 2 * Q, 3 * Q)
         interleave(V, staging[:, 0 : Q * PACK // 2], w_first[:, :, 0 : Q // 2])
         gather(3, 3 * Q, S)
         quantize(0, 0, 2 * Q)

@@ -36,12 +36,9 @@ def tile_list_hboth_none_kernel(tc, xT, w, wgt, wgo, offs, offs2, out):
         wgo_all = held.tile([P, S], F32, name="wgo_all")
         planes = [held.tile([P, T], F32, name=f"plane{i}") for i in range(PACK)]
         windows = [held.tile([P, T], F32, name=f"window{b}") for b in range(WINDOWS)]
-        gathered_row = held.tile([P, PACK * S + 4 * Q - Q // 2], F32, align_bytes=64, name="gathered")
-        gathered = gathered_row[:, 0 : PACK * S].rearrange("p (t j) -> p t j", t=PACK)
-        w_first = gathered_row[:, PACK * S - Q // 2 : PACK * S + 4 * Q - Q // 2].rearrange("p (t n) -> p t n", t=PACK)
-        w_raw = [w_first] + [
-            held.tile([P, PACK, width], F32, name=f"w_raw{c0}")[:] for c0, width in W_LOADS[1:]
-        ]
+        gathered_row = held.tile([P, PACK * S], F32, align_bytes=64, name="gathered")
+        gathered = gathered_row[:].rearrange("p (t j) -> p t j", t=PACK)
+        w_raw = [held.tile([P, PACK, width], F32, name=f"w_raw{c0}")[:] for c0, width in W_LOADS]
         staging = held.tile([P, 4 * Q * PACK], BF16, align_bytes=64, name="staging")
         codes = held.tile([P, S + M], U32, align_bytes=64, name="codes")
         scales = held.tile([P, S + M], U8, align_bytes=64, name="scales")
@@ -152,18 +149,18 @@ def tile_list_hboth_none_kernel(tc, xT, w, wgt, wgo, offs, offs2, out):
         V, A = nc.vector.tensor_copy, nc.scalar.copy
         gather(0, 0, S)
         gather(1, 0, S)
-        interleave_pair(0, 1, 0, 3 * Q)
+        interleave_pair(0, 0, 0, Q)
+        interleave_pair(0, 2, Q, 3 * Q)
         gather(2, 0, S)
         gather(3, 0, Q)
-        gather(3, Q, 2 * Q)
-        gather(3, 2 * Q, 3 * Q)
-        interleave_pair(2, 1, 0, Q)
-        interleave(A, staging[:, Q * PACK // 2 : Q * PACK], w_first[:, :, Q // 2 : Q])
+        gather(3, Q, S)
+        interleave_pair(2, 0, 0, Q)
+        interleave(A, stage(1, 2)[:, 0 : Q * PACK // 2], w_raw[0][:, :, 0 : Q // 2])
+        interleave(V, stage(1, 2)[:, Q * PACK // 2 :], w_raw[0][:, :, Q // 2 : Q])
         interleave_pair(2, 2, Q, 2 * Q)
         interleave_pair(2, 3, 2 * Q, 3 * Q)
-        interleave(V, staging[:, 0 : Q * PACK // 2], w_first[:, :, 0 : Q // 2])
-        gather(3, 3 * Q, S)
-        quantize(0, 0, 2 * Q)
+        quantize(0, Q, 2 * Q)
+        quantize(1, 0, Q)
         product(0, 0, Q, 0)
         interleave_x(V, 1, 3 * Q)
         quantize(2, 2 * Q, 4 * Q)

@@ -14,17 +14,20 @@ MULT = mybir.AluOpType.mult
 P = 128
 PACK = 4
 GROUP = 16
-BLOCKS = M // P
+LINE = 4
+STRIPS = M // P
+Q = 128
+SLOT = Q * PACK
+SLOTS = 4
 WINDOWS = 3
 BANKS = 8
-Q = 128
-W_LOADS = ((0, 128), (128, 128), (256, 256), (512, 512))
+W_LOADS = ((0, Q), (Q, Q), (2 * Q, 2 * Q), (4 * Q, 4 * Q))
 
 
 def tile_list_hboth_none_kernel(tc, xT, w, wgt, wgo, offs, offs2, out):
     nc = tc.nc
-    x_planes = xT.rearrange("(p i) t -> p i t", i=PACK)
-    w_rows = w.rearrange("(p i) n -> p i n", i=PACK)
+    x_planes = xT.rearrange("(p t) token -> p t token", t=PACK)
+    w_rows = w.rearrange("(p t) n -> p t n", t=PACK)
 
     with (
         tc.tile_pool(name="held", bufs=1) as held,
@@ -34,107 +37,107 @@ def tile_list_hboth_none_kernel(tc, xT, w, wgt, wgo, offs, offs2, out):
         list_out = held.tile([P, S // GROUP], U16, name="list_out")
         wgt_all = held.tile([P, S], F32, name="wgt_all")
         wgo_all = held.tile([P, S], F32, name="wgo_all")
-        planes = [held.tile([P, T], F32, name=f"plane{i}") for i in range(PACK)]
-        windows = [held.tile([P, T], F32, name=f"window{b}") for b in range(WINDOWS)]
+        planes = [held.tile([P, T], F32, name=f"plane{t}") for t in range(PACK)]
+        windows = [held.tile([P, T], F32, name=f"window{n}") for n in range(WINDOWS)]
         gathered_row = held.tile([P, PACK * S], F32, align_bytes=64, name="gathered")
         gathered = gathered_row[:].rearrange("p (t j) -> p t j", t=PACK)
-        w_raw = [held.tile([P, PACK, width], F32, name=f"w_raw{c0}")[:] for c0, width in W_LOADS]
-        staging = held.tile([P, 4 * Q * PACK], BF16, align_bytes=64, name="staging")
+        w_raw = [held.tile([P, PACK, width], F32, name=f"w_raw{first}")[:] for first, width in W_LOADS]
+        staging = held.tile([P, SLOTS * SLOT], BF16, align_bytes=64, name="staging")
         codes = held.tile([P, S + M], U32, align_bytes=64, name="codes")
         scales = held.tile([P, S + M], U8, align_bytes=64, name="scales")
-        y = {b: held.tile([P, S], F32, name=f"y{b}") for b in range(BLOCKS) if b != 3}
+        y = {b: held.tile([P, S], F32, name=f"y{b}") for b in range(STRIPS) if b != 3}
 
-        def stage(u0, u1):
-            return staging[:, u0 * Q * PACK : u1 * Q * PACK]
+        def slots(first, count):
+            return staging[:, first * SLOT : (first + count) * SLOT]
 
-        def x_cols(j0, j1):
-            return slice(Q + j0, Q + j1)
+        def x_col(j):
+            return Q + j
 
-        def w_cols(n0, n1):
-            shift = 0 if n0 == 0 else S
-            return slice(shift + n0, shift + n1)
+        def w_col(strip):
+            return 0 if strip == 0 else S + strip * Q
 
-        def y_part(b, j0, j1):
-            if b == 3:
+        def y_part(strip, j0, j1):
+            if strip == 3:
                 return w_raw[3][:, 3, :]
-            if (b, j0) == (1, 2 * Q):
+            if (strip, j0) == (1, 2 * Q):
                 return w_raw[2][:, 3, :]
-            if (b, j0) == (0, 3 * Q):
+            if (strip, j0) == (0, 3 * Q):
                 return w_raw[2][:, 2, Q : 2 * Q]
-            return y[b][:, j0:j1]
+            return y[strip][:, j0:j1]
 
-        def load_w(n):
-            c0, width = W_LOADS[n]
-            nc.sync.dma_start(w_raw[n], w_rows[:, :, c0 : c0 + width])
+        def load_w(number):
+            first, width = W_LOADS[number]
+            nc.sync.dma_start(w_raw[number], w_rows[:, :, first : first + width])
 
         def entries(list_tile, j0, j1):
             return list_tile[:, j0 // GROUP : j1 // GROUP]
 
-        def gather(i, j0, j1):
+        def gather(t, j0, j1):
             nc.vector.tensor_tensor(
-                gathered[:, i, j0:j1],
-                planes[i][:].indirect(entries(list_in, j0, j1)),
+                gathered[:, t, j0:j1],
+                planes[t][:].indirect(entries(list_in, j0, j1)),
                 wgt_all[:, j0:j1],
                 MULT,
             )
 
+        def by_lines_out(staged):
+            return staged.rearrange("p (c i t) -> p c t i", i=LINE, t=PACK)
+
+        def by_lines_in(rows):
+            return rows.rearrange("p t (c i) -> p c t i", i=LINE)
+
         def interleave(copy, staged, rows):
-            copy(
-                out=staged.rearrange("p (c i t) -> p c t i", i=4, t=PACK),
-                in_=rows.rearrange("p t (c i) -> p c t i", i=4),
-            )
+            copy(out=by_lines_out(staged), in_=by_lines_in(rows))
 
-        def interleave_x(copy, unit, j0):
-            interleave(copy, stage(unit, unit + 1), gathered[:, :, j0 : j0 + Q])
-
-        def interleave_pair(t0, unit, j0, j1):
+        def interleave_pair(t, slot, j0, j1):
             nc.scalar.copy(
-                out=stage(unit, unit + (j1 - j0) // Q).rearrange("p (c i t) -> p c t i", i=4, t=PACK)[:, :, t0 : t0 + 2, :],
-                in_=gathered[:, t0 : t0 + 2, j0:j1].rearrange("p t (c i) -> p c t i", i=4),
+                out=by_lines_out(slots(slot, (j1 - j0) // Q))[:, :, t : t + 2, :],
+                in_=by_lines_in(gathered[:, t : t + 2, j0:j1]),
             )
 
-        def interleave_w(copy, unit, n0, n1):
-            n = max(m for m in range(len(W_LOADS)) if W_LOADS[m][0] <= n0)
-            c0 = W_LOADS[n][0]
-            interleave(copy, stage(unit, unit + (n1 - n0) // Q), w_raw[n][:, :, n0 - c0 : n1 - c0])
+        def interleave_w(slot, strip, count):
+            number = max(n for n, (first, width) in enumerate(W_LOADS) if first <= strip * Q)
+            column = strip * Q - W_LOADS[number][0]
+            interleave(nc.scalar.copy, slots(slot, count), w_raw[number][:, :, column : column + count * Q])
 
-        def quantize(unit, c0, c1):
+        def quantize(slot, count, column):
             nc.vector.quantize_mx(
-                out=codes[:, c0:c1].bitcast(FP8X4),
-                scales=scales[:, c0:c1],
-                in_=stage(unit, unit + (c1 - c0) // Q),
+                out=codes[:, column : column + count * Q].bitcast(FP8X4),
+                scales=scales[:, column : column + count * Q],
+                in_=slots(slot, count),
             )
 
-        def product(b, j0, j1, bank_number):
-            bank = psum.tile([P, j1 - j0], F32, name=f"bank{bank_number % BANKS}")
-            rows = w_cols(b * P, (b + 1) * P)
+        def product(strip, j0, j1, number):
+            bank = psum.tile([P, j1 - j0], F32, name=f"bank{number % BANKS}")
+            w_cols = slice(w_col(strip), w_col(strip) + Q)
+            x_cols = slice(x_col(j0), x_col(j1))
             nc.tensor.matmul_mx(
                 out=bank[:],
-                lhsT=codes[:, rows].bitcast(FP8X4),
-                lhsT_scale=scales[:, rows],
-                rhs=codes[:, x_cols(j0, j1)].bitcast(FP8X4),
-                rhs_scale=scales[:, x_cols(j0, j1)],
+                lhsT=codes[:, w_cols].bitcast(FP8X4),
+                lhsT_scale=scales[:, w_cols],
+                rhs=codes[:, x_cols].bitcast(FP8X4),
+                rhs_scale=scales[:, x_cols],
                 start=True,
                 stop=True,
             )
-            nc.scalar.copy(out=y_part(b, j0, j1), in_=bank[:])
+            nc.scalar.copy(out=y_part(strip, j0, j1), in_=bank[:])
 
-        def scatter(b, j0, j1):
+        def scatter(strip, j0, j1):
             nc.vector.tensor_tensor(
-                windows[b % WINDOWS][:].indirect(entries(list_out, j0, j1)),
-                y_part(b, j0, j1),
+                windows[strip % WINDOWS][:].indirect(entries(list_out, j0, j1)),
+                y_part(strip, j0, j1),
                 wgo_all[:, j0:j1],
                 MULT,
             )
 
-        def store(b):
-            nc.sync.dma_start(out[b * P : (b + 1) * P, :], windows[b % WINDOWS][:])
+        def store(strip):
+            nc.sync.dma_start(out[strip * P : (strip + 1) * P, :], windows[strip % WINDOWS][:])
 
         nc.sync.dma_start(planes[0][:], x_planes[:, 0, :])
         nc.scalar.dma_start(wgt_all[:], wgt)
         nc.sync.dma_start(list_in[:], offs)
-        for i in range(1, PACK):
-            nc.sync.dma_start(planes[i][:], x_planes[:, i, :])
+        for t in range(1, PACK):
+            nc.sync.dma_start(planes[t][:], x_planes[:, t, :])
         load_w(0)
         nc.sync.dma_start(list_out[:], offs2)
         nc.sync.dma_start(wgo_all[:, 0 : 3 * Q], wgo[:, 0 : 3 * Q])
@@ -146,50 +149,53 @@ def tile_list_hboth_none_kernel(tc, xT, w, wgt, wgo, offs, offs2, out):
         for window in windows:
             nc.vector.memset(window[:], 0.0)
 
-        V, A = nc.vector.tensor_copy, nc.scalar.copy
         gather(0, 0, S)
         gather(1, 0, S)
         interleave_pair(0, 0, 0, Q)
         interleave_pair(0, 2, Q, 3 * Q)
         gather(2, 0, S)
         gather(3, 0, Q)
-        gather(3, Q, S)
+        gather(3, Q, 2 * Q)
+        gather(3, 2 * Q, S)
         interleave_pair(2, 0, 0, Q)
-        interleave(A, stage(1, 2)[:, 0 : Q * PACK // 2], w_raw[0][:, :, 0 : Q // 2])
-        interleave(V, stage(1, 2)[:, Q * PACK // 2 :], w_raw[0][:, :, Q // 2 : Q])
+        interleave(nc.scalar.copy, slots(1, 1)[:, 0 : SLOT // 2], w_raw[0][:, :, 0 : Q // 2])
+        interleave(nc.vector.tensor_copy, slots(1, 1)[:, SLOT // 2 :], w_raw[0][:, :, Q // 2 : Q])
         interleave_pair(2, 2, Q, 2 * Q)
         interleave_pair(2, 3, 2 * Q, 3 * Q)
-        quantize(0, Q, 2 * Q)
-        quantize(1, 0, Q)
+        quantize(0, 1, x_col(0))
+        quantize(1, 1, w_col(0))
         product(0, 0, Q, 0)
-        interleave_x(V, 1, 3 * Q)
-        quantize(2, 2 * Q, 4 * Q)
-        interleave_w(A, 2, Q, 2 * Q)
+
+        interleave(nc.vector.tensor_copy, slots(1, 1), gathered[:, :, 3 * Q : S])
+        quantize(2, 2, x_col(Q))
+        interleave_w(2, 1, 1)
         product(0, Q, 3 * Q, 1)
+
         scatter(0, 0, Q)
-        quantize(1, 4 * Q, 6 * Q)
+        quantize(1, 2, x_col(3 * Q))
         scatter(0, Q, 3 * Q)
         product(1, 0, 2 * Q, 2)
-        interleave_w(A, 1, 2 * Q, 3 * Q)
-        interleave_w(A, 2, 3 * Q, 4 * Q)
+        interleave_w(1, 2, 1)
+        interleave_w(2, 3, 1)
         product(0, 3 * Q, S, 3)
         product(1, 2 * Q, S, 4)
         scatter(1, 0, 2 * Q)
-        quantize(1, 6 * Q, 8 * Q)
+        quantize(1, 2, w_col(2))
         scatter(0, 3 * Q, S)
         store(0)
         product(2, 0, S, 5)
-        interleave_w(A, 0, 4 * Q, 6 * Q)
-        interleave_w(A, 2, 6 * Q, 8 * Q)
+        interleave_w(0, 4, 2)
+        interleave_w(2, 6, 2)
         product(3, 0, S, 6)
         scatter(1, 2 * Q, S)
         store(1)
         scatter(2, 0, S)
         store(2)
-        quantize(0, 8 * Q, 12 * Q)
+        quantize(0, 4, w_col(4))
         product(4, 0, S, 7)
-        for b in range(3, BLOCKS):
-            if b + 2 < BLOCKS:
-                product(b + 2, 0, S, b + 5)
-            scatter(b, 0, S)
-            store(b)
+
+        for strip in range(3, STRIPS):
+            if strip + 2 < STRIPS:
+                product(strip + 2, 0, S, strip + 5)
+            scatter(strip, 0, S)
+            store(strip)

@@ -14,6 +14,7 @@ MULT = mybir.AluOpType.mult
 P = 128
 PACK = 4
 GROUP = 16
+BLOCK = 32
 LINE = 4
 STRIPS = M // P
 Q = 128
@@ -35,10 +36,13 @@ def tile_list_hboth_none_kernel(tc, xT, w, wgt, wgo, offs, offs2, out):
     ):
         list_in = held.tile([P, S // GROUP], U16, name="list_in")
         list_out = held.tile([P, S // GROUP], U16, name="list_out")
-        wgt_all = held.tile([P, S], F32, name="wgt_all")
+        wgt_cut = held.tile([P, BLOCK], F32, align_bytes=64, name="wgt_cut")
+        wgt_turned = held.tile([P, BLOCK], F32, align_bytes=64, name="last_window")
+        wgt_spread = held.tile([P, S], F32, align_bytes=64, name="wgt_spread")
+        wgt_all = held.tile([P, S], F32, align_bytes=64, name="wgt_all")
         wgo_all = held.tile([P, S], F32, name="wgo_all")
         planes = [held.tile([P, T], F32, name=f"plane{t}") for t in range(PACK)]
-        windows = [held.tile([P, T], F32, name=f"window{n}") for n in range(WINDOWS)]
+        windows = [held.tile([P, T], F32, name=f"window{n}") for n in range(WINDOWS - 1)]
         gathered_row = held.tile([P, PACK * S], F32, align_bytes=64, name="gathered")
         gathered = gathered_row[:].rearrange("p (t j) -> p t j", t=PACK)
         w_raw = [held.tile([P, PACK, width], F32, name=f"w_raw{first}")[:] for first, width in W_LOADS]
@@ -133,8 +137,8 @@ def tile_list_hboth_none_kernel(tc, xT, w, wgt, wgo, offs, offs2, out):
         def store(strip):
             nc.sync.dma_start(out[strip * P : (strip + 1) * P, :], windows[strip % WINDOWS][:])
 
+        nc.sync.dma_start(wgt_cut[:], wgt.rearrange("(g r) (b i) -> g r b i", r=GROUP, i=BLOCK)[:, 0])
         nc.sync.dma_start(planes[0][:], x_planes[:, 0, :])
-        nc.scalar.dma_start(wgt_all[:], wgt)
         nc.sync.dma_start(list_in[:], offs)
         for t in range(1, PACK):
             nc.sync.dma_start(planes[t][:], x_planes[:, t, :])
@@ -146,10 +150,22 @@ def tile_list_hboth_none_kernel(tc, xT, w, wgt, wgo, offs, offs2, out):
         nc.sync.dma_start(wgo_all[:, 3 * Q : S], wgo[:, 3 * Q : S])
         load_w(3)
 
-        for window in windows:
-            nc.vector.memset(window[:], 0.0)
+        nc.vector.memset(windows[0][:], 0.0)
+        nc.vector.memset(windows[1][:], 0.0)
 
-        gather(0, 0, S)
+        nc.vector.transpose(wgt_turned[:], wgt_cut[:])
+        pieces = wgt_turned[:].rearrange("p (h b) -> p b h", h=2).unsqueeze(3).to_broadcast([P, GROUP, 2, GROUP])
+        spread = wgt_spread[:].rearrange("p (b h c) -> p b h c", h=2, c=GROUP)
+        for half in range(2):
+            nc.vector.tensor_copy(spread[:, half * 8 : half * 8 + 8], pieces[:, half * 8 : half * 8 + 8])
+        windows.append(held.tile([P, T], F32, align_bytes=64, name="last_window"))
+        nc.gpsimd.memset(windows[2][:], 0.0)
+        for half in range(2):
+            columns = slice(half * S // 2, (half + 1) * S // 2)
+            nc.vector.transpose(wgt_all[:, columns], wgt_spread[:, columns])
+
+        gather(0, 0, S // 2)
+        gather(0, S // 2, S)
         gather(1, 0, S)
         interleave_pair(0, 0, 0, Q)
         interleave_pair(0, 2, Q, 3 * Q)

import concourse.mybir as mybir

K, M, T, S = 512, 1024, 1024, 512
FLOPS = 2 * K * M * S

F32 = mybir.dt.float32
BF16 = mybir.dt.bfloat16
U32 = mybir.dt.uint32
U16 = mybir.dt.uint16
U8 = mybir.dt.uint8
FP8X4 = mybir.dt.float8_e4m3fn_x4
MULT = mybir.AluOpType.mult

P = 128
PACK = 4
GROUP = 16
BLOCK = 32
LINE = 4
STRIPS = M // P
Q = 128
SLOT = Q * PACK
SLOTS = 4
WINDOWS = 3
BANKS = 8
W_LOADS = ((0, Q), (Q, Q), (2 * Q, 2 * Q), (4 * Q, 4 * Q))


def tile_list_hboth_none_kernel(tc, xT, w, wgt, wgo, offs, offs2, out):
    nc = tc.nc
    x_planes = xT.rearrange("(p t) token -> p t token", t=PACK)
    w_rows = w.rearrange("(p t) n -> p t n", t=PACK)

    with (
        tc.tile_pool(name="held", bufs=1) as held,
        tc.psum_pool(name="psum", bufs=1) as psum,
    ):
        list_in = held.tile([P, S // GROUP], U16, name="list_in")
        list_out = held.tile([P, S // GROUP], U16, name="list_out")
        wgt_cut = held.tile([P, BLOCK], F32, align_bytes=64, name="wgt_cut")
        wgt_turned = held.tile([P, BLOCK], F32, align_bytes=64, name="last_window")
        wgt_spread = held.tile([P, S], F32, align_bytes=64, name="wgt_spread")
        wgt_all = held.tile([P, S], F32, align_bytes=64, name="wgt_all")
        wgo_all = held.tile([P, S], F32, name="wgo_all")
        planes = [held.tile([P, T], F32, name=f"plane{t}") for t in range(PACK)]
        windows = [held.tile([P, T], F32, name=f"window{n}") for n in range(WINDOWS - 1)]
        gathered_row = held.tile([P, PACK * S], F32, align_bytes=64, name="gathered")
        gathered = gathered_row[:].rearrange("p (t j) -> p t j", t=PACK)
        w_raw = [held.tile([P, PACK, width], F32, name=f"w_raw{first}")[:] for first, width in W_LOADS]
        staging = held.tile([P, SLOTS * SLOT], BF16, align_bytes=64, name="staging")
        codes = held.tile([P, S + M], U32, align_bytes=64, name="codes")
        scales = held.tile([P, S + M], U8, align_bytes=64, name="scales")
        y = {b: held.tile([P, S], F32, name=f"y{b}") for b in range(STRIPS) if b != 3}

        def slots(first, count):
            return staging[:, first * SLOT : (first + count) * SLOT]

        def x_col(j):
            return Q + j

        def w_col(strip):
            return 0 if strip == 0 else S + strip * Q

        def y_part(strip, j0, j1):
            if strip == 3:
                return w_raw[3][:, 3, :]
            if (strip, j0) == (1, 2 * Q):
                return w_raw[2][:, 3, :]
            if (strip, j0) == (0, 3 * Q):
                return w_raw[2][:, 2, Q : 2 * Q]
            return y[strip][:, j0:j1]

        def load_w(number):
            first, width = W_LOADS[number]
            nc.sync.dma_start(w_raw[number], w_rows[:, :, first : first + width])

        def entries(list_tile, j0, j1):
            return list_tile[:, j0 // GROUP : j1 // GROUP]

        def gather(t, j0, j1):
            nc.vector.tensor_tensor(
                gathered[:, t, j0:j1],
                planes[t][:].indirect(entries(list_in, j0, j1)),
                wgt_all[:, j0:j1],
                MULT,
            )

        def by_lines_out(staged):
            return staged.rearrange("p (c i t) -> p c t i", i=LINE, t=PACK)

        def by_lines_in(rows):
            return rows.rearrange("p t (c i) -> p c t i", i=LINE)

        def interleave(copy, staged, rows):
            copy(out=by_lines_out(staged), in_=by_lines_in(rows))

        def interleave_pair(t, slot, j0, j1):
            nc.scalar.copy(
                out=by_lines_out(slots(slot, (j1 - j0) // Q))[:, :, t : t + 2, :],
                in_=by_lines_in(gathered[:, t : t + 2, j0:j1]),
            )

        def interleave_w(slot, strip, count):
            number = max(n for n, (first, width) in enumerate(W_LOADS) if first <= strip * Q)
            column = strip * Q - W_LOADS[number][0]
            interleave(nc.scalar.copy, slots(slot, count), w_raw[number][:, :, column : column + count * Q])

        def quantize(slot, count, column):
            nc.vector.quantize_mx(
                out=codes[:, column : column + count * Q].bitcast(FP8X4),
                scales=scales[:, column : column + count * Q],
                in_=slots(slot, count),
            )

        def product(strip, j0, j1, number):
            bank = psum.tile([P, j1 - j0], F32, name=f"bank{number % BANKS}")
            w_cols = slice(w_col(strip), w_col(strip) + Q)
            x_cols = slice(x_col(j0), x_col(j1))
            nc.tensor.matmul_mx(
                out=bank[:],
                lhsT=codes[:, w_cols].bitcast(FP8X4),
                lhsT_scale=scales[:, w_cols],
                rhs=codes[:, x_cols].bitcast(FP8X4),
                rhs_scale=scales[:, x_cols],
                start=True,
                stop=True,
            )
            nc.scalar.copy(out=y_part(strip, j0, j1), in_=bank[:])

        def scatter(strip, j0, j1):
            nc.vector.tensor_tensor(
                windows[strip % WINDOWS][:].indirect(entries(list_out, j0, j1)),
                y_part(strip, j0, j1),
                wgo_all[:, j0:j1],
                MULT,
            )

        def store(strip):
            nc.sync.dma_start(out[strip * P : (strip + 1) * P, :], windows[strip % WINDOWS][:])

        nc.sync.dma_start(wgt_cut[:], wgt.rearrange("(g r) (b i) -> g r b i", r=GROUP, i=BLOCK)[:, 0])
        nc.sync.dma_start(planes[0][:], x_planes[:, 0, :])
        nc.sync.dma_start(list_in[:], offs)
        for t in range(1, PACK):
            nc.sync.dma_start(planes[t][:], x_planes[:, t, :])
        load_w(0)
        nc.sync.dma_start(list_out[:], offs2)
        nc.sync.dma_start(wgo_all[:, 0 : 3 * Q], wgo[:, 0 : 3 * Q])
        load_w(1)
        load_w(2)
        nc.sync.dma_start(wgo_all[:, 3 * Q : S], wgo[:, 3 * Q : S])
        load_w(3)

        nc.vector.memset(windows[0][:], 0.0)
        nc.vector.memset(windows[1][:], 0.0)

        nc.vector.transpose(wgt_turned[:], wgt_cut[:])
        pieces = wgt_turned[:].rearrange("p (h b) -> p b h", h=2).unsqueeze(3).to_broadcast([P, GROUP, 2, GROUP])
        spread = wgt_spread[:].rearrange("p (b h c) -> p b h c", h=2, c=GROUP)
        for half in range(2):
            nc.vector.tensor_copy(spread[:, half * 8 : half * 8 + 8], pieces[:, half * 8 : half * 8 + 8])
        windows.append(held.tile([P, T], F32, align_bytes=64, name="last_window"))
        nc.gpsimd.memset(windows[2][:], 0.0)
        for half in range(2):
            columns = slice(half * S // 2, (half + 1) * S // 2)
            nc.vector.transpose(wgt_all[:, columns], wgt_spread[:, columns])

        gather(0, 0, S // 2)
        gather(0, S // 2, S)
        gather(1, 0, S)
        interleave_pair(0, 0, 0, Q)
        interleave_pair(0, 2, Q, 3 * Q)
        gather(2, 0, S)
        gather(3, 0, Q)
        gather(3, Q, 2 * Q)
        gather(3, 2 * Q, S)
        interleave_pair(2, 0, 0, Q)
        interleave(nc.scalar.copy, slots(1, 1)[:, 0 : SLOT // 2], w_raw[0][:, :, 0 : Q // 2])
        interleave(nc.vector.tensor_copy, slots(1, 1)[:, SLOT // 2 :], w_raw[0][:, :, Q // 2 : Q])
        interleave_pair(2, 2, Q, 2 * Q)
        interleave_pair(2, 3, 2 * Q, 3 * Q)
        quantize(0, 1, x_col(0))
        quantize(1, 1, w_col(0))
        product(0, 0, Q, 0)

        interleave(nc.vector.tensor_copy, slots(1, 1), gathered[:, :, 3 * Q : S])
        quantize(2, 2, x_col(Q))
        interleave_w(2, 1, 1)
        product(0, Q, 3 * Q, 1)

        scatter(0, 0, Q)
        quantize(1, 2, x_col(3 * Q))
        scatter(0, Q, 3 * Q)
        product(1, 0, 2 * Q, 2)
        interleave_w(1, 2, 1)
        interleave_w(2, 3, 1)
        product(0, 3 * Q, S, 3)
        product(1, 2 * Q, S, 4)
        scatter(1, 0, 2 * Q)
        quantize(1, 2, w_col(2))
        scatter(0, 3 * Q, S)
        store(0)
        product(2, 0, S, 5)
        interleave_w(0, 4, 2)
        interleave_w(2, 6, 2)
        product(3, 0, S, 6)
        scatter(1, 2 * Q, S)
        store(1)
        scatter(2, 0, S)
        store(2)
        quantize(0, 4, w_col(4))
        product(4, 0, S, 7)

        for strip in range(3, STRIPS):
            if strip + 2 < STRIPS:
                product(strip + 2, 0, S, strip + 5)
            scatter(strip, 0, S)
            store(strip)
